import numpy as np
import ml_dtypes


def mxq(x, axis, fmt="e4m3"):
    dtype, down = {"e4m3": (ml_dtypes.float8_e4m3fn, 7), "e5m2": (ml_dtypes.float8_e5m2, 14)}[fmt]
    v = np.moveaxis(np.asarray(x, np.float32).astype(ml_dtypes.bfloat16).astype(np.float64), axis, -1)
    blocks = v.reshape(v.shape[:-1] + (-1, 32))
    amax = np.abs(blocks).max(-1, keepdims=True)
    byte = np.maximum(np.where(amax > 0, np.frexp(amax)[1] - 1 + 127, 0) - down, 1)
    scale = np.exp2(byte - 127.0)
    codes = (blocks / scale).astype(np.float32).astype(dtype).astype(np.float64)
    return np.moveaxis((codes * scale).reshape(v.shape), -1, axis)


WIDE = False


def mx_kscale(k):
    if not WIDE:
        return np.ones(k)
    levels = np.array([10, -10, 5, -5, 0])
    if k % 512:
        return np.exp2(np.random.permutation(np.resize(levels, k // 32))).repeat(32)
    a = np.empty((k // 512, 16))
    for p in range(k // 512):
        a[p, :8] = np.random.permutation(np.resize(levels, 8))
        for g in range(8):
            far = levels[np.abs(levels - a[p, g]) >= 10]
            a[p, g + 8] = far[np.random.randint(len(far))]
    return np.exp2(a.ravel()).repeat(32)


def f64(x):
    return np.asarray(x).astype(np.float64)


def striped8(idx):
    return np.asarray(idx).reshape(8, -1, 16).transpose(0, 2, 1).reshape(128, -1).astype(np.uint16)


def unstriped8(offs):
    return offs.reshape(8, 16, -1).transpose(0, 2, 1).reshape(8, -1).astype(np.int64)


def pick8(x, idx, run):
    r = np.arange(len(x))
    return x[r[:, None], idx[r % (8 * run) // run]]


E2M1 = np.array([0.0, 0.5, 1.0, 1.5, 2.0, 3.0, 4.0, 6.0, -0.0, -0.5, -1.0, -1.5, -2.0, -3.0, -4.0, -6.0])


def pack_weight(w, fmt):
    k, n = w.shape
    w = f64(np.asarray(w, np.float32).astype(ml_dtypes.bfloat16)).reshape(k // 32, 32, n)
    amax = np.abs(w).max(1)
    if fmt == "e4m3":
        byte = np.frexp(amax)[1] - 1 + 127 - 7
    else:
        mant, ex = np.frexp(amax / 6.0)
        byte = np.where(mant > 0.5, ex, ex - 1) + 127
    byte = np.clip(np.where(amax > 0, byte, 1), 1, 254)
    scaled = (w * np.exp2(127.0 - byte)[:, None, :]).reshape(k, n).astype(np.float32)
    by_word = np.ascontiguousarray(scaled.reshape(k // 512, 128, 4, n).transpose(0, 1, 3, 2))
    if fmt == "e4m3":
        words = by_word.astype(ml_dtypes.float8_e4m3fn).view(np.uint8)
    else:
        c = by_word.astype(ml_dtypes.float4_e2m1fn).view(np.uint8) & 0xF
        words = (c[..., 0::2] | (c[..., 1::2] << 4)).reshape(k // 512, 128, 2 * n)
    return np.ascontiguousarray(words), np.ascontiguousarray(byte.astype(np.uint8).reshape(k // 512, 16, n))


def unpack_weight(words, scales, fmt):
    g, _, n = scales.shape
    words = np.ascontiguousarray(words).reshape(g, 128, n, -1)
    if fmt == "e4m3":
        vals = words.view(ml_dtypes.float8_e4m3fn).astype(np.float64)
    else:
        nib = np.empty((g, 128, n, 4), np.uint8)
        nib[..., 0::2] = words & 0xF
        nib[..., 1::2] = words >> 4
        vals = E2M1[nib]
    vals = vals * np.repeat(np.exp2(scales.astype(np.float64) - 127.0), 8, axis=1)[..., None]
    return vals.transpose(0, 1, 3, 2).reshape(g * 512, n)


D, T, U, I, Q = 512, 1024, 1024, 512, 128


def setup_inputs():
    n = np.random.standard_normal
    idx = np.stack([np.random.permutation(U)[:I] for _ in range(8)])
    idx2 = np.stack([np.random.permutation(U)[:I] for _ in range(8)])
    idx3 = np.stack([np.random.permutation(U)[:I] for _ in range(8)])
    idx4 = np.stack([np.random.permutation(T)[:I] for _ in range(8)])
    idx5 = np.stack([np.random.permutation(U)[:I] for _ in range(8)])
    idx6 = np.stack([np.random.permutation(U)[:I] for _ in range(8)])
    fd = mx_kscale(D)
    cachep = pack_weight(n((D, T)) / fd[:, None], "e2m1")
    draftp = pack_weight(n((D, U)) / fd[:, None], "e4m3")
    return {
        "query": (n((D, Q)) * 1.0 / np.sqrt(D) * fd[:, None]).astype(np.float32),
        "cache_words": cachep[0],
        "cache_scales": cachep[1],
        "draft_words": draftp[0],
        "draft_scales": draftp[1],
        "offs": striped8(idx),
        "offs2": striped8(idx2),
        "offs3": striped8(idx3),
        "offs4": striped8(idx4),
        "offs5": striped8(idx5),
        "offs6": striped8(idx6),
    }


def reference(query, cache_words, cache_scales, draft_words, draft_scales, offs, offs2, offs3, offs4, offs5, offs6):
    idx = unstriped8(offs)
    idx2 = unstriped8(offs2)
    idx3 = unstriped8(offs3)
    idx4 = unstriped8(offs4)
    idx5 = unstriped8(offs5)
    idx6 = unstriped8(offs6)
    cacheu = unpack_weight(cache_words, cache_scales, "e2m1")
    draftu = unpack_weight(draft_words, draft_scales, "e4m3")
    queryq = mxq(f64(query), 0, "e4m3")
    a = queryq.T @ cacheu
    b = queryq.T @ draftu
    nb = np.zeros((Q, U))
    nb[np.arange(Q)[:, None], idx2[np.arange(Q) % 128 // 16]] = pick8(b, idx, 16)
    n2 = np.zeros((Q, U))
    n2[np.arange(Q)[:, None], idx5[np.arange(Q) % 128 // 16]] = pick8(nb, idx3, 16)
    m1 = np.maximum(n2, b)
    w = pick8(m1, idx6, 16) + pick8(a, idx4, 16)
    y = w - pick8(nb, idx3, 16)
    return y

@@ -1,0 +1,154 @@
+from contextlib import ExitStack
+
+import concourse.mybir as mybir
+
+D, T, U, I, Q = 512, 1024, 1024, 512, 128
+FLOPS = 2 * D * Q * (T + U)
+
+F32 = mybir.dt.float32
+BF16 = mybir.dt.bfloat16
+I32 = mybir.dt.int32
+U32 = mybir.dt.uint32
+U16 = mybir.dt.uint16
+U8 = mybir.dt.uint8
+FP8X4 = mybir.dt.float8_e4m3fn_x4
+FP4X4 = mybir.dt.float4_e2m1fn_x4
+ALU = mybir.AluOpType
+COPY = mybir.ActivationFunctionType.Copy
+
+P = 128
+PACK = 4
+HALF = I // 2
+LIST_COLS = I // 16
+HALF_COLS = LIST_COLS // 2
+B_TILE = 256
+A_TILE = 512
+DRAFT_CHUNK = 512
+
+
+def load_scale_plane(nc, plane, scales):
+    for quad in range(4):
+        nc.sync.dma_start(
+            out=plane[32 * quad : 32 * quad + 4, :].bitcast(I32),
+            in_=scales[0, 4 * quad : 4 * quad + 4, :].bitcast(I32),
+        )
+
+
+def tile_attend_parentpath_two_kernel(
+    tc, query, cache_words, cache_scales, draft_words, draft_scales, offs, offs2, offs3, offs4, offs5, offs6, out
+):
+    nc = tc.nc
+    with ExitStack() as ctx:
+        lists = ctx.enter_context(tc.tile_pool(name="lists", bufs=1))
+        sb = ctx.enter_context(tc.tile_pool(name="sb", bufs=1))
+        psum = ctx.enter_context(tc.psum_pool(name="psum", bufs=1))
+
+        def load_list(name, source):
+            tile = lists.tile([P, LIST_COLS], U16, name=name)
+            nc.sync.dma_start(tile[:], source)
+            return tile
+
+        def half_of(tile, h):
+            return tile[:, h * HALF_COLS : (h + 1) * HALF_COLS]
+
+        def slots(h):
+            return slice(h * HALF, (h + 1) * HALF)
+
+        draft_plane = sb.tile([P, U], U8, align_bytes=64)
+        nc.vector.memset(draft_plane[:].bitcast(I32), 0)
+
+        q_raw = sb.tile([P, PACK, Q], F32)
+        nc.sync.dma_start(out=q_raw[:], in_=query.rearrange("(p j) q -> p j q", j=PACK))
+        load_scale_plane(nc, draft_plane, draft_scales)
+        draft_rows = draft_words[0].rearrange("p n t -> p (n t)")
+        draft_codes = []
+        for c in range(U // DRAFT_CHUNK):
+            codes = sb.tile([P, DRAFT_CHUNK], U32, name="draft_codes%d" % c, align_bytes=64)
+            nc.sync.dma_start(
+                out=codes[:].bitcast(I32),
+                in_=draft_rows[:, PACK * DRAFT_CHUNK * c : PACK * DRAFT_CHUNK * (c + 1)].bitcast(I32),
+            )
+            draft_codes.append(codes)
+        parents1 = load_list("parents1", offs)
+        children1 = load_list("children1", offs2)
+        parents2 = load_list("parents2", offs3)
+        children2 = load_list("children2", offs5)
+
+        nb = sb.tile([P, U], F32)
+        nc.vector.memset(nb[:], 0.0)
+        cache_plane = sb.tile([P, T], U8, align_bytes=64)
+        nc.vector.memset(cache_plane[:].bitcast(I32), 0)
+        n2 = sb.tile([P, U], F32)
+        nc.gpsimd.memset(n2[:], 0.0)
+
+        cache_codes = sb.tile([P, 2 * T], U8, align_bytes=64)
+        nc.sync.dma_start(out=cache_codes[:].bitcast(I32), in_=cache_words[0].bitcast(I32))
+        load_scale_plane(nc, cache_plane, cache_scales)
+        cache_picks = load_list("cache_picks", offs4)
+        final_picks = load_list("final_picks", offs6)
+
+        q_grouped = sb.tile([P, Q, PACK], BF16, align_bytes=64)
+        nc.vector.tensor_copy(out=q_grouped[:], in_=q_raw[:].rearrange("p j q -> p q j"))
+        q_codes = sb.tile([P, Q], U32, align_bytes=64)
+        q_plane = sb.tile([P, Q], U8, align_bytes=64)
+        nc.vector.quantize_mx(
+            out=q_codes[:].bitcast(FP8X4), scales=q_plane[:], in_=q_grouped[:].rearrange("p q j -> p (q j)")
+        )
+
+        b = sb.tile([P, U], F32)
+        for n in range(U // B_TILE):
+            cols = slice(n * B_TILE, (n + 1) * B_TILE)
+            c, first = divmod(n * B_TILE, DRAFT_CHUNK)
+            bank = psum.tile([Q, B_TILE], F32, name="b_bank%d" % n, tag="bank%d" % n)
+            nc.tensor.matmul_mx(
+                out=bank[:],
+                lhsT=q_codes[:].bitcast(FP8X4),
+                lhsT_scale=q_plane[:],
+                rhs=draft_codes[c][:, first : first + B_TILE].bitcast(FP8X4),
+                rhs_scale=draft_plane[:, cols],
+                start=True,
+                stop=True,
+            )
+            if n % 2 == 0:
+                nc.scalar.activation(b[:, cols], bank[:], COPY)
+            else:
+                nc.vector.tensor_copy(b[:, cols], bank[:])
+
+        b_picked = sb.tile([P, I], F32)
+        for h in range(2):
+            nc.vector.tensor_copy(b_picked[:, slots(h)], b[:].indirect(half_of(parents1, h)))
+        for h in range(2):
+            nc.scalar.activation(nb[:].indirect(half_of(children1, h)), b_picked[:, slots(h)], COPY)
+
+        nb_picked = sb.tile([P, I], F32)
+        for h in range(2):
+            nc.vector.tensor_copy(nb_picked[:, slots(h)], nb[:].indirect(half_of(parents2, h)))
+        for h in range(2):
+            nc.scalar.activation(n2[:].indirect(half_of(children2, h)), nb_picked[:, slots(h)], COPY)
+
+        a = sb.tile([P, T], F32, tag="a_then_m1")
+        for n in range(T // A_TILE):
+            cols = slice(n * A_TILE, (n + 1) * A_TILE)
+            bank = psum.tile([Q, A_TILE], F32, name="a_bank%d" % n, tag="bank%d" % (2 + n))
+            nc.tensor.matmul_mx(
+                out=bank[:],
+                lhsT=q_codes[:].bitcast(FP8X4),
+                lhsT_scale=q_plane[:],
+                rhs=cache_codes[:, 2 * n * A_TILE : 2 * (n + 1) * A_TILE].bitcast(FP4X4),
+                rhs_scale=cache_plane[:, cols],
+                start=True,
+                stop=True,
+            )
+            nc.vector.tensor_copy(a[:, cols], bank[:])
+        rest = sb.tile([P, I], F32)
+        nc.vector.tensor_tensor(rest[:], a[:].indirect(cache_picks[:]), nb_picked[:], ALU.subtract)
+
+        m1 = sb.tile([P, U], F32, tag="a_then_m1")
+        nc.vector.tensor_tensor(m1[:], n2[:], b[:], ALU.max)
+
+        result = sb.tile([P, I], F32)
+        for h in range(2):
+            nc.vector.tensor_tensor(
+                result[:, slots(h)], m1[:].indirect(half_of(final_picks, h)), rest[:, slots(h)], ALU.add
+            )
+            nc.sync.dma_start(out=out[:, slots(h)], in_=result[:, slots(h)])

@@ -21,7 +21,7 @@ PACK = 4
 HALF = I // 2
 LIST_COLS = I // 16
 HALF_COLS = LIST_COLS // 2
-B_TILE = 256
+B_TILES = (256, 256, 256, 128, 128)
 A_TILE = 512
 DRAFT_CHUNK = 512
 
@@ -59,7 +59,6 @@ def tile_attend_parentpath_two_kernel(
 
         q_raw = sb.tile([P, PACK, Q], F32)
         nc.sync.dma_start(out=q_raw[:], in_=query.rearrange("(p j) q -> p j q", j=PACK))
-        load_scale_plane(nc, draft_plane, draft_scales)
         draft_rows = draft_words[0].rearrange("p n t -> p (n t)")
         draft_codes = []
         for c in range(U // DRAFT_CHUNK):
@@ -69,6 +68,8 @@ def tile_attend_parentpath_two_kernel(
                 in_=draft_rows[:, PACK * DRAFT_CHUNK * c : PACK * DRAFT_CHUNK * (c + 1)].bitcast(I32),
             )
             draft_codes.append(codes)
+            if c == 0:
+                load_scale_plane(nc, draft_plane, draft_scales)
         parents1 = load_list("parents1", offs)
         children1 = load_list("children1", offs2)
         parents2 = load_list("parents2", offs3)
@@ -79,7 +80,7 @@ def tile_attend_parentpath_two_kernel(
         cache_plane = sb.tile([P, T], U8, align_bytes=64)
         nc.vector.memset(cache_plane[:].bitcast(I32), 0)
         n2 = sb.tile([P, U], F32)
-        nc.gpsimd.memset(n2[:], 0.0)
+        nc.vector.memset(n2[:], 0.0)
 
         cache_codes = sb.tile([P, 2 * T], U8, align_bytes=64)
         nc.sync.dma_start(out=cache_codes[:].bitcast(I32), in_=cache_words[0].bitcast(I32))
@@ -88,7 +89,11 @@ def tile_attend_parentpath_two_kernel(
         final_picks = load_list("final_picks", offs6)
 
         q_grouped = sb.tile([P, Q, PACK], BF16, align_bytes=64)
-        nc.vector.tensor_copy(out=q_grouped[:], in_=q_raw[:].rearrange("p j q -> p q j"))
+        q_dst = q_grouped[:].rearrange("p (c i) j -> p c j i", i=4)
+        q_src = q_raw[:].rearrange("p j (c i) -> p c j i", i=4)
+        split = Q // 8
+        nc.vector.tensor_copy(out=q_dst[:, :split], in_=q_src[:, :split])
+        nc.scalar.activation(q_dst[:, split:], q_src[:, split:], COPY)
         q_codes = sb.tile([P, Q], U32, align_bytes=64)
         q_plane = sb.tile([P, Q], U8, align_bytes=64)
         nc.vector.quantize_mx(
@@ -96,15 +101,16 @@ def tile_attend_parentpath_two_kernel(
         )
 
         b = sb.tile([P, U], F32)
-        for n in range(U // B_TILE):
-            cols = slice(n * B_TILE, (n + 1) * B_TILE)
-            c, first = divmod(n * B_TILE, DRAFT_CHUNK)
-            bank = psum.tile([Q, B_TILE], F32, name="b_bank%d" % n, tag="bank%d" % n)
+        for n, width in enumerate(B_TILES):
+            start = sum(B_TILES[:n])
+            cols = slice(start, start + width)
+            c, first = divmod(start, DRAFT_CHUNK)
+            bank = psum.tile([Q, width], F32, name="b_bank%d" % n, tag="bank%d" % n)
             nc.tensor.matmul_mx(
                 out=bank[:],
                 lhsT=q_codes[:].bitcast(FP8X4),
                 lhsT_scale=q_plane[:],
-                rhs=draft_codes[c][:, first : first + B_TILE].bitcast(FP8X4),
+                rhs=draft_codes[c][:, first : first + width].bitcast(FP8X4),
                 rhs_scale=draft_plane[:, cols],
                 start=True,
                 stop=True,
@@ -115,21 +121,19 @@ def tile_attend_parentpath_two_kernel(
                 nc.vector.tensor_copy(b[:, cols], bank[:])
 
         b_picked = sb.tile([P, I], F32)
-        for h in range(2):
-            nc.vector.tensor_copy(b_picked[:, slots(h)], b[:].indirect(half_of(parents1, h)))
-        for h in range(2):
-            nc.scalar.activation(nb[:].indirect(half_of(children1, h)), b_picked[:, slots(h)], COPY)
+        nc.vector.tensor_copy(b_picked[:, slots(0)], b[:].indirect(half_of(parents1, 0)))
+        nc.scalar.activation(b_picked[:, slots(1)], b[:].indirect(half_of(parents1, 1)), COPY)
+        nc.scalar.activation(nb[:].indirect(children1[:]), b_picked[:], COPY)
 
         nb_picked = sb.tile([P, I], F32)
-        for h in range(2):
-            nc.vector.tensor_copy(nb_picked[:, slots(h)], nb[:].indirect(half_of(parents2, h)))
-        for h in range(2):
-            nc.scalar.activation(n2[:].indirect(half_of(children2, h)), nb_picked[:, slots(h)], COPY)
+        nc.vector.tensor_copy(nb_picked[:, slots(0)], nb[:].indirect(half_of(parents2, 0)))
+        nc.scalar.activation(nb_picked[:, slots(1)], nb[:].indirect(half_of(parents2, 1)), COPY)
+        nc.scalar.activation(n2[:].indirect(children2[:]), nb_picked[:], COPY)
 
         a = sb.tile([P, T], F32, tag="a_then_m1")
         for n in range(T // A_TILE):
             cols = slice(n * A_TILE, (n + 1) * A_TILE)
-            bank = psum.tile([Q, A_TILE], F32, name="a_bank%d" % n, tag="bank%d" % (2 + n))
+            bank = psum.tile([Q, A_TILE], F32, name="a_bank%d" % n, tag="bank%d" % (3 + n))
             nc.tensor.matmul_mx(
                 out=bank[:],
                 lhsT=q_codes[:].bitcast(FP8X4),
@@ -147,8 +151,11 @@ def tile_attend_parentpath_two_kernel(
         nc.vector.tensor_tensor(m1[:], n2[:], b[:], ALU.max)
 
         result = sb.tile([P, I], F32)
-        for h in range(2):
-            nc.vector.tensor_tensor(
-                result[:, slots(h)], m1[:].indirect(half_of(final_picks, h)), rest[:, slots(h)], ALU.add
-            )
-            nc.sync.dma_start(out=out[:, slots(h)], in_=result[:, slots(h)])
+        m1_picked = sb.tile([P, HALF], F32)
+        nc.scalar.activation(m1_picked[:], m1[:].indirect(half_of(final_picks, 1)), COPY)
+        nc.vector.tensor_tensor(
+            result[:, slots(0)], m1[:].indirect(half_of(final_picks, 0)), rest[:, slots(0)], ALU.add
+        )
+        nc.sync.dma_start(out=out[:, slots(0)], in_=result[:, slots(0)])
+        nc.vector.tensor_tensor(result[:, slots(1)], m1_picked[:], rest[:, slots(1)], ALU.add)
+        nc.sync.dma_start(out=out[:, slots(1)], in_=result[:, slots(1)])

from contextlib import ExitStack

import concourse.mybir as mybir

D, T, U, I, Q = 512, 1024, 1024, 512, 128
FLOPS = 2 * D * Q * (T + U)

F32 = mybir.dt.float32
BF16 = mybir.dt.bfloat16
I32 = mybir.dt.int32
U32 = mybir.dt.uint32
U16 = mybir.dt.uint16
U8 = mybir.dt.uint8
FP8X4 = mybir.dt.float8_e4m3fn_x4
FP4X4 = mybir.dt.float4_e2m1fn_x4
ALU = mybir.AluOpType
COPY = mybir.ActivationFunctionType.Copy

P = 128
PACK = 4
HALF = I // 2
LIST_COLS = I // 16
HALF_COLS = LIST_COLS // 2
B_TILES = (256, 256, 256, 128, 128)
A_TILE = 512
DRAFT_CHUNK = 512


def load_scale_plane(nc, plane, scales):
    for quad in range(4):
        nc.sync.dma_start(
            out=plane[32 * quad : 32 * quad + 4, :].bitcast(I32),
            in_=scales[0, 4 * quad : 4 * quad + 4, :].bitcast(I32),
        )


def tile_attend_parentpath_two_kernel(
    tc, query, cache_words, cache_scales, draft_words, draft_scales, offs, offs2, offs3, offs4, offs5, offs6, out
):
    nc = tc.nc
    with ExitStack() as ctx:
        lists = ctx.enter_context(tc.tile_pool(name="lists", bufs=1))
        sb = ctx.enter_context(tc.tile_pool(name="sb", bufs=1))
        psum = ctx.enter_context(tc.psum_pool(name="psum", bufs=1))

        def load_list(name, source):
            tile = lists.tile([P, LIST_COLS], U16, name=name)
            nc.sync.dma_start(tile[:], source)
            return tile

        def half_of(tile, h):
            return tile[:, h * HALF_COLS : (h + 1) * HALF_COLS]

        def slots(h):
            return slice(h * HALF, (h + 1) * HALF)

        draft_plane = sb.tile([P, U], U8, align_bytes=64)
        nc.vector.memset(draft_plane[:].bitcast(I32), 0)

        q_raw = sb.tile([P, PACK, Q], F32)
        nc.sync.dma_start(out=q_raw[:], in_=query.rearrange("(p j) q -> p j q", j=PACK))
        draft_rows = draft_words[0].rearrange("p n t -> p (n t)")
        draft_codes = []
        for c in range(U // DRAFT_CHUNK):
            codes = sb.tile([P, DRAFT_CHUNK], U32, name="draft_codes%d" % c, align_bytes=64)
            nc.sync.dma_start(
                out=codes[:].bitcast(I32),
                in_=draft_rows[:, PACK * DRAFT_CHUNK * c : PACK * DRAFT_CHUNK * (c + 1)].bitcast(I32),
            )
            draft_codes.append(codes)
            if c == 0:
                load_scale_plane(nc, draft_plane, draft_scales)
        parents1 = load_list("parents1", offs)
        children1 = load_list("children1", offs2)
        parents2 = load_list("parents2", offs3)
        children2 = load_list("children2", offs5)

        nb = sb.tile([P, U], F32)
        nc.vector.memset(nb[:], 0.0)
        cache_plane = sb.tile([P, T], U8, align_bytes=64)
        nc.vector.memset(cache_plane[:].bitcast(I32), 0)
        n2 = sb.tile([P, U], F32)
        nc.vector.memset(n2[:], 0.0)

        cache_codes = sb.tile([P, 2 * T], U8, align_bytes=64)
        nc.sync.dma_start(out=cache_codes[:].bitcast(I32), in_=cache_words[0].bitcast(I32))
        load_scale_plane(nc, cache_plane, cache_scales)
        cache_picks = load_list("cache_picks", offs4)
        final_picks = load_list("final_picks", offs6)

        q_grouped = sb.tile([P, Q, PACK], BF16, align_bytes=64)
        q_dst = q_grouped[:].rearrange("p (c i) j -> p c j i", i=4)
        q_src = q_raw[:].rearrange("p j (c i) -> p c j i", i=4)
        split = Q // 8
        nc.vector.tensor_copy(out=q_dst[:, :split], in_=q_src[:, :split])
        nc.scalar.activation(q_dst[:, split:], q_src[:, split:], COPY)
        q_codes = sb.tile([P, Q], U32, align_bytes=64)
        q_plane = sb.tile([P, Q], U8, align_bytes=64)
        nc.vector.quantize_mx(
            out=q_codes[:].bitcast(FP8X4), scales=q_plane[:], in_=q_grouped[:].rearrange("p q j -> p (q j)")
        )

        b = sb.tile([P, U], F32)
        for n, width in enumerate(B_TILES):
            start = sum(B_TILES[:n])
            cols = slice(start, start + width)
            c, first = divmod(start, DRAFT_CHUNK)
            bank = psum.tile([Q, width], F32, name="b_bank%d" % n, tag="bank%d" % n)
            nc.tensor.matmul_mx(
                out=bank[:],
                lhsT=q_codes[:].bitcast(FP8X4),
                lhsT_scale=q_plane[:],
                rhs=draft_codes[c][:, first : first + width].bitcast(FP8X4),
                rhs_scale=draft_plane[:, cols],
                start=True,
                stop=True,
            )
            if n % 2 == 0:
                nc.scalar.activation(b[:, cols], bank[:], COPY)
            else:
                nc.vector.tensor_copy(b[:, cols], bank[:])

        b_picked = sb.tile([P, I], F32)
        nc.vector.tensor_copy(b_picked[:, slots(0)], b[:].indirect(half_of(parents1, 0)))
        nc.scalar.activation(b_picked[:, slots(1)], b[:].indirect(half_of(parents1, 1)), COPY)
        nc.scalar.activation(nb[:].indirect(children1[:]), b_picked[:], COPY)

        nb_picked = sb.tile([P, I], F32)
        nc.vector.tensor_copy(nb_picked[:, slots(0)], nb[:].indirect(half_of(parents2, 0)))
        nc.scalar.activation(nb_picked[:, slots(1)], nb[:].indirect(half_of(parents2, 1)), COPY)
        nc.scalar.activation(n2[:].indirect(children2[:]), nb_picked[:], COPY)

        a = sb.tile([P, T], F32, tag="a_then_m1")
        for n in range(T // A_TILE):
            cols = slice(n * A_TILE, (n + 1) * A_TILE)
            bank = psum.tile([Q, A_TILE], F32, name="a_bank%d" % n, tag="bank%d" % (3 + n))
            nc.tensor.matmul_mx(
                out=bank[:],
                lhsT=q_codes[:].bitcast(FP8X4),
                lhsT_scale=q_plane[:],
                rhs=cache_codes[:, 2 * n * A_TILE : 2 * (n + 1) * A_TILE].bitcast(FP4X4),
                rhs_scale=cache_plane[:, cols],
                start=True,
                stop=True,
            )
            nc.vector.tensor_copy(a[:, cols], bank[:])
        rest = sb.tile([P, I], F32)
        nc.vector.tensor_tensor(rest[:], a[:].indirect(cache_picks[:]), nb_picked[:], ALU.subtract)

        m1 = sb.tile([P, U], F32, tag="a_then_m1")
        nc.vector.tensor_tensor(m1[:], n2[:], b[:], ALU.max)

        result = sb.tile([P, I], F32)
        m1_picked = sb.tile([P, HALF], F32)
        nc.scalar.activation(m1_picked[:], m1[:].indirect(half_of(final_picks, 1)), COPY)
        nc.vector.tensor_tensor(
            result[:, slots(0)], m1[:].indirect(half_of(final_picks, 0)), rest[:, slots(0)], ALU.add
        )
        nc.sync.dma_start(out=out[:, slots(0)], in_=result[:, slots(0)])
        nc.vector.tensor_tensor(result[:, slots(1)], m1_picked[:], rest[:, slots(1)], ALU.add)
        nc.sync.dma_start(out=out[:, slots(1)], in_=result[:, slots(1)])
